import numpy as np
import ml_dtypes


def mxq(x, axis, fmt="e4m3"):
    dtype, down = {"e4m3": (ml_dtypes.float8_e4m3fn, 7), "e5m2": (ml_dtypes.float8_e5m2, 14)}[fmt]
    v = np.moveaxis(np.asarray(x, np.float32).astype(ml_dtypes.bfloat16).astype(np.float64), axis, -1)
    blocks = v.reshape(v.shape[:-1] + (-1, 32))
    amax = np.abs(blocks).max(-1, keepdims=True)
    byte = np.maximum(np.where(amax > 0, np.frexp(amax)[1] - 1 + 127, 0) - down, 1)
    scale = np.exp2(byte - 127.0)
    codes = (blocks / scale).astype(np.float32).astype(dtype).astype(np.float64)
    return np.moveaxis((codes * scale).reshape(v.shape), -1, axis)


WIDE = False


def mx_kscale(k):
    if not WIDE:
        return np.ones(k)
    levels = np.array([10, -10, 5, -5, 0])
    if k % 512:
        return np.exp2(np.random.permutation(np.resize(levels, k // 32))).repeat(32)
    a = np.empty((k // 512, 16))
    for p in range(k // 512):
        a[p, :8] = np.random.permutation(np.resize(levels, 8))
        for g in range(8):
            far = levels[np.abs(levels - a[p, g]) >= 10]
            a[p, g + 8] = far[np.random.randint(len(far))]
    return np.exp2(a.ravel()).repeat(32)


def f64(x):
    return np.asarray(x).astype(np.float64)


def striped(idx):
    return np.tile(idx.reshape(-1, 16).T, (8, 1)).astype(np.uint16)


def unstriped(offs):
    return offs[:16].T.reshape(-1).astype(np.int64)


def pack_weight(w):
    k, n = w.shape
    w = f64(np.asarray(w, np.float32).astype(ml_dtypes.bfloat16)).reshape(k // 32, 32, n)
    amax = np.abs(w).max(1)
    byte = np.clip(np.where(amax > 0, np.frexp(amax)[1] - 1 + 127 - 7, 1), 1, 254)
    scaled = (w * np.exp2(127.0 - byte)[:, None, :]).reshape(k, n).astype(np.float32)
    words = np.ascontiguousarray(scaled.reshape(k // 512, 128, 4, n).transpose(0, 1, 3, 2)).astype(ml_dtypes.float8_e4m3fn).view(np.uint8)
    return words, np.ascontiguousarray(byte.astype(np.uint8).reshape(k // 512, 16, n))


def unpack_weight(words, scales):
    g, p, n, _ = words.shape
    vals = np.ascontiguousarray(words).view(ml_dtypes.float8_e4m3fn).astype(np.float64) * np.repeat(np.exp2(scales.astype(np.float64) - 127.0), 8, axis=1)[..., None]
    return vals.transpose(0, 1, 3, 2).reshape(g * 512, n)


E2M1 = np.array([0.0, 0.5, 1.0, 1.5, 2.0, 3.0, 4.0, 6.0, -0.0, -0.5, -1.0, -1.5, -2.0, -3.0, -4.0, -6.0])


def pack_fp4(w):
    k, n = w.shape
    w = f64(np.asarray(w, np.float32).astype(ml_dtypes.bfloat16)).reshape(k // 32, 32, n)
    amax = np.abs(w).max(1)
    mant, ex = np.frexp(amax / 6.0)
    byte = np.clip(np.where(amax > 0, np.where(mant > 0.5, ex, ex - 1) + 127, 1), 1, 254)
    scaled = (w * np.exp2(127.0 - byte)[:, None, :]).reshape(k, n).astype(np.float32)
    c = np.ascontiguousarray(scaled.reshape(k // 512, 128, 4, n).transpose(0, 1, 3, 2)).astype(ml_dtypes.float4_e2m1fn).view(np.uint8) & 0xF
    words = (c[..., 0::2] | (c[..., 1::2] << 4)).reshape(k // 512, 128, 2 * n)
    return np.ascontiguousarray(words), np.ascontiguousarray(byte.astype(np.uint8).reshape(k // 512, 16, n))


def unpack_fp4(words, scales):
    g, _, n = scales.shape
    words = np.ascontiguousarray(words).reshape(g, 128, n, 2)
    nib = np.empty((g, 128, n, 4), np.uint8)
    nib[..., 0::2] = words & 0xF
    nib[..., 1::2] = words >> 4
    vals = E2M1[nib] * np.repeat(np.exp2(scales.astype(np.float64) - 127.0), 8, axis=1)[..., None]
    return vals.transpose(0, 1, 3, 2).reshape(g * 512, n)


def planes(y):
    n, m = y.shape
    v = y.astype(np.float32).astype(ml_dtypes.bfloat16).astype(np.float64).reshape(n // 32, 32, m)
    top = np.abs(v).max(1)
    byte = np.clip(np.where(top > 0, np.frexp(top)[1] - 1 + 127 - 7, 1), 1, 254)
    codes = (v * np.exp2(127.0 - byte)[:, None, :]).reshape(n, m).astype(np.float32).astype(ml_dtypes.float8_e4m3fn).view(np.uint8)
    words = codes.reshape(n // 512, 128, 4, m).transpose(0, 1, 3, 2)
    return np.ascontiguousarray(words), np.ascontiguousarray(byte.astype(np.uint8).reshape(n // 512, 16, m))


def sigmoid(v):
    return 1.0 / (1.0 + np.exp(-np.maximum(v, -700.0)))


K, T, S, N, H = 512, 2048, 512, 512, 512


def setup_inputs():
    n = np.random.standard_normal
    s = mx_kscale(K)[:, None]
    u = mx_kscale(H)
    packed_xT = pack_weight(n((K, T)) * s)
    packed_w1 = pack_fp4(n((K, N)) / np.sqrt(K) / s)
    packed_w2 = pack_fp4(n((K, N)) / np.sqrt(K) / s)
    packed_w3 = pack_fp4(n((H, N)) / np.sqrt(H) / u[:, None])
    return {
        "x_words": packed_xT[0],
        "x_scales": packed_xT[1],
        "w1_words": packed_w1[0],
        "w1_scales": packed_w1[1],
        "w2_words": packed_w2[0],
        "w2_scales": packed_w2[1],
        "unit": (np.random.uniform(0.6, 1.4, (H, 1)) * u[:, None]).astype(np.float32),
        "w3_words": packed_w3[0],
        "w3_scales": packed_w3[1],
        "offs": striped(np.random.permutation(T)[:S]),
        "s1": striped(np.random.permutation(S)),
        "s2": striped(np.random.permutation(S)),
    }


def reference(x_words, x_scales, w1_words, w1_scales, w2_words, w2_scales, unit, w3_words, w3_scales, offs, s1, s2):
    xq = unpack_weight(x_words, x_scales)[:, unstriped(offs)]
    yg = unpack_fp4(w2_words, w2_scales).T @ xq
    set1 = sigmoid(1.5 * yg)
    set2 = set1[:, unstriped(s2)]
    y = unpack_fp4(w1_words, w1_scales).T @ xq
    y1 = y[:, unstriped(s1)]
    lay1 = set1 * y + (-1.0 * set1 + 1.0) * y1
    x12 = lay1[:, unstriped(s2)]
    lay2 = set2 * lay1 + (-1.0 * set2 + 1.0) * x12
    x21 = lay2[:, unstriped(s1)]
    hid = f64(unit) * (lay2 * (x21 + 0.5))
    out_0 = unpack_fp4(w3_words, w3_scales).T @ mxq(hid, 0, "e4m3")
    return (out_0,) + planes(out_0)

@@ -1,0 +1,200 @@
+from contextlib import ExitStack
+
+import concourse.mybir as mybir
+
+K, T, S, N = 512, 2048, 512, 512
+FLOPS = 3 * 2 * 512 * 512 * 512
+
+F32 = mybir.dt.float32
+BF16 = mybir.dt.bfloat16
+I32 = mybir.dt.int32
+U32 = mybir.dt.uint32
+U16 = mybir.dt.uint16
+U8 = mybir.dt.uint8
+FP8X4 = mybir.dt.float8_e4m3fn_x4
+FP4X4 = mybir.dt.float4_e2m1fn_x4
+ALU = mybir.AluOpType
+ACT = mybir.ActivationFunctionType
+
+P = 128
+PACK = 4
+SPARE = 32
+CH = 128
+NCH = S // CH
+
+
+def load_scale_rows(queue, tile_bytes, dram_rows):
+    for q in range(4):
+        queue.dma_start(
+            out=tile_bytes[32 * q : 32 * q + 4, :].bitcast(I32),
+            in_=dram_rows[4 * q : 4 * q + 4, :].bitcast(I32),
+        )
+
+
+def tile_picked_ybenesn_mul_po_kernel(
+    tc, x_words, x_scales, w1_words, w1_scales, w2_words, w2_scales, unit, w3_words, w3_scales, offs, s1, s2,
+    out_0, out_1, out_2,
+):
+    nc = tc.nc
+    with ExitStack() as ctx:
+        keep = ctx.enter_context(tc.tile_pool(name="keep", bufs=1))
+        psum = ctx.enter_context(tc.psum_pool(name="psum", bufs=1))
+
+        offs_sb = keep.tile([P, S // 16], U16, name="offs_sb")
+        s1_sb = keep.tile([P, S // 16], U16, name="s1_sb")
+        s2_sb = keep.tile([P, S // 16], U16, name="s2_sb")
+        xw_all = keep.tile([P, T], U32, name="xw_all", align_bytes=64)
+        xs_all = keep.tile([P, T], U8, name="xs_all", align_bytes=64)
+        raw_words = [keep.tile([P, 2 * N], U8, name=f"raw_words{i}", align_bytes=64) for i in range(2)]
+        raw_scales = [keep.tile([P, N], U8, name=f"raw_scales{i}", align_bytes=64) for i in range(2)]
+        unit_sb = keep.tile([P, PACK], F32, name="unit_sb")
+
+        y_wins = [keep.tile([P, S + SPARE], F32, name=f"y_win{t}") for t in range(PACK)]
+        set_wins = [keep.tile([P, S + SPARE], F32, name=f"set_win{t}") for t in range(PACK)]
+        nc.vector.memset(xs_all[:].bitcast(I32), 0)
+        nc.vector.memset(raw_scales[0][:].bitcast(I32), 0)
+        for win in y_wins + set_wins:
+            nc.gpsimd.memset(win[:, S : S + SPARE], 0.0)
+        nc.gpsimd.dma_start(out=unit_sb[:], in_=unit.rearrange("(p t) o -> p (t o)", t=PACK))
+        nc.gpsimd.memset(raw_scales[1][:].bitcast(I32), 0)
+
+        nc.sync.dma_start(offs_sb[:], offs)
+        nc.sync.dma_start(out=raw_words[0][:].bitcast(I32), in_=w1_words[0].bitcast(I32))
+        nc.sync.dma_start(out=raw_words[1][:].bitcast(I32), in_=w2_words[0].bitcast(I32))
+        nc.sync.dma_start(s1_sb[:], s1)
+        nc.sync.dma_start(s2_sb[:], s2)
+        nc.sync.dma_start(out=xw_all[:].bitcast(I32), in_=x_words[0].rearrange("p n t -> p (n t)").bitcast(I32))
+        load_scale_rows(nc.scalar, xs_all, x_scales[0])
+        load_scale_rows(nc.sync, raw_scales[0], w1_scales[0])
+        load_scale_rows(nc.sync, raw_scales[1], w2_scales[0])
+
+        def deal_words(raw, name):
+            dealt = keep.tile([P, 2 * N], U8, name=name, align_bytes=64)
+            nc.scalar.copy(
+                out=dealt[:].bitcast(U16).rearrange("p (t m) -> p t m", t=PACK),
+                in_=raw[:].bitcast(U16).rearrange("p (m t) -> p t m", t=PACK),
+            )
+            return dealt
+
+        def deal_scales(raw, name):
+            dealt = keep.tile([P, N], U8, name=name, align_bytes=64)
+            nc.vector.tensor_copy(
+                out=dealt[:].rearrange("p (t m) -> p t m", t=PACK),
+                in_=raw[:].rearrange("p (m t) -> p t m", t=PACK),
+            )
+            return dealt
+
+        w1w = deal_words(raw_words[0], "w1w")
+        w2w = deal_words(raw_words[1], "w2w")
+
+        xw = keep.tile([P, S], U32, name="xw", align_bytes=64)
+        xs = keep.tile([P, S], U8, name="xs", align_bytes=64)
+        nc.vector.tensor_copy(xs[:], xs_all[:].indirect(offs_sb[:]))
+        w1s = deal_scales(raw_scales[0], "w1s")
+        nc.vector.tensor_copy(xw[:], xw_all[:].indirect(offs_sb[:]))
+        w2s = deal_scales(raw_scales[1], "w2s")
+
+        nc.sync.dma_start(out=raw_words[0][:].bitcast(I32), in_=w3_words[0].bitcast(I32))
+        load_scale_rows(nc.sync, raw_scales[0], w3_scales[0])
+
+        def product(bank, words, scales, t, rhs, rhs_scale):
+            nc.tensor.matmul_mx(
+                out=bank,
+                lhsT=words[:, 2 * P * t : 2 * P * (t + 1)].bitcast(FP4X4),
+                lhsT_scale=scales[:, P * t : P * (t + 1)],
+                rhs=rhs.bitcast(FP8X4),
+                rhs_scale=rhs_scale,
+                start=True,
+                stop=True,
+            )
+
+        neg_lay2 = keep.tile([P, PACK, S], F32, name="neg_lay2")
+        picked = keep.tile([P, PACK, S], F32, name="picked")
+        w3w = None
+        w3s = None
+        for t in range(PACK):
+            yg_ps = psum.tile([P, S], F32, name=f"yg_ps{t}", tag=f"bank{2 * t}")
+            y_ps = psum.tile([P, S], F32, name=f"y_ps{t}", tag=f"bank{2 * t + 1}")
+            product(y_ps[:], w1w, w1s, t, xw[:], xs[:])
+            product(yg_ps[:], w2w, w2s, t, xw[:], xs[:])
+
+            y_win, set_win = y_wins[t], set_wins[t]
+            part_tile = keep.tile([P, S], F32, name=f"part{t}")
+            rest_win = keep.tile([P, 2 * S], F32, name=f"rest_win{t}")
+            last_win = keep.tile([P, 2 * S], F32, name=f"last_win{t}")
+            lay1 = keep.tile([P, S], F32, name=f"lay1_{t}")
+            kept = keep.tile([P, S], F32, name=f"kept{t}")
+            y, set1 = y_win[:, 0:S], set_win[:, 0:S]
+            y1, diff, part = last_win[:, S : 2 * S], rest_win[:, S : 2 * S], part_tile[:]
+
+            if t == 0:
+                half = S // 2
+                nc.vector.tensor_copy(out=y, in_=y_ps[:])
+                nc.scalar.activation(set1, yg_ps[:], ACT.Sigmoid, scale=1.5)
+                nc.vector.tensor_copy(y1[:, 0:half], y_win[:].indirect(s1_sb[:, 0 : half // 16]))
+                nc.scalar.activation(y1[:, half:S], y_win[:].indirect(s1_sb[:, half // 16 : S // 16]), ACT.Copy)
+            else:
+                nc.scalar.copy(out=y, in_=y_ps[:])
+                nc.scalar.activation(y1, y_win[:].indirect(s1_sb[:]), ACT.Copy)
+                nc.scalar.activation(set1, yg_ps[:], ACT.Sigmoid, scale=1.5)
+
+            nc.vector.tensor_tensor(diff, y, y1, ALU.subtract)
+            nc.vector.tensor_tensor(part, diff, set1, ALU.mult)
+            nc.vector.tensor_tensor(lay1[:], part, y1, ALU.add)
+
+            nc.vector.scalar_tensor_tensor(rest_win[:, 0:S], set1, 1.0, lay1[:], ALU.subtract, ALU.mult)
+            if t == 0:
+                nc.vector.tensor_tensor(kept[:], set_win[:].indirect(s2_sb[:]), lay1[:], ALU.mult)
+            else:
+                set2 = keep.tile([P, S], F32, name=f"set2_{t}")
+                nc.scalar.activation(set2[:], set_win[:].indirect(s2_sb[:]), ACT.Copy)
+                nc.vector.tensor_tensor(kept[:], set2[:], lay1[:], ALU.mult)
+            nc.vector.tensor_tensor(neg_lay2[:, t, :], rest_win[:].indirect(s2_sb[:]), kept[:], ALU.subtract)
+            nc.vector.tensor_scalar(last_win[:, 0:S], neg_lay2[:, t, :], -0.5, unit_sb[:, t : t + 1], ALU.add, ALU.mult)
+            width = CH if t == PACK - 1 else S
+            for c0 in range(0, S, width):
+                cols = s1_sb[:, c0 // 16 : (c0 + width) // 16]
+                nc.scalar.activation(picked[:, t, c0 : c0 + width], last_win[:].indirect(cols), ACT.Copy)
+            if t == 0:
+                w3w = deal_words(raw_words[0], "w3w")
+                w3s = deal_scales(raw_scales[0], "w3s")
+
+        out_words = keep.tile([P, S], U32, name="out_words", align_bytes=64)
+        out_scales = keep.tile([P, S], U8, name="out_scales", align_bytes=64)
+        out_rows = out_0.rearrange("(p t) j -> p t j", t=PACK)
+        out_word_rows = out_1[0].rearrange("p n t -> p (n t)").bitcast(I32)
+        results = []
+        for c in range(NCH):
+            cols = slice(c * CH, (c + 1) * CH)
+            hid = keep.tile([P, CH * PACK], BF16, name=f"hid{c}", align_bytes=64)
+            nc.vector.tensor_tensor(
+                hid[:].rearrange("p (g i t) -> p g t i", i=4, t=PACK),
+                picked[:, :, cols].rearrange("p t (g i) -> p g t i", i=4),
+                neg_lay2[:, :, cols].rearrange("p t (g i) -> p g t i", i=4),
+                ALU.mult,
+            )
+            hid_words = keep.tile([P, CH], U32, name=f"hid_words{c}", align_bytes=64)
+            hid_scales = keep.tile([P, CH], U8, name=f"hid_scales{c}", align_bytes=64)
+            nc.vector.quantize_mx(out=hid_words[:].bitcast(FP8X4), scales=hid_scales[:], in_=hid[:])
+            out_ps = psum.tile([P, PACK, CH], F32, name=f"out_ps{c}", tag=f"bank{c}")
+            for t in range(PACK):
+                product(out_ps[:, t, :], w3w, w3s, t, hid_words[:], hid_scales[:])
+            out_f32 = keep.tile([P, PACK, CH], F32, name=f"out_f32_{c}")
+            nc.scalar.copy(out=out_f32[:], in_=out_ps[:])
+            nc.sync.dma_start(out=out_rows[:, :, cols], in_=out_f32[:])
+            results.append(out_f32)
+        for c in range(NCH):
+            cols = slice(c * CH, (c + 1) * CH)
+            out_f32 = results[c]
+            out_bf = keep.tile([P, CH * PACK], BF16, name=f"out_bf{c}", align_bytes=64)
+            nc.vector.tensor_copy(
+                out=out_bf[:].rearrange("p (g i t) -> p g t i", i=4, t=PACK),
+                in_=out_f32[:].rearrange("p t (g i) -> p g t i", i=4),
+            )
+            nc.vector.quantize_mx(out=out_words[:, cols].bitcast(FP8X4), scales=out_scales[:, cols], in_=out_bf[:])
+            nc.sync.dma_start(out=out_word_rows[:, cols], in_=out_words[:, cols].bitcast(I32))
+        for q in range(4):
+            nc.sync.dma_start(
+                out=out_2[0][4 * q : 4 * q + 4, :].bitcast(I32),
+                in_=out_scales[32 * q : 32 * q + 4, :].bitcast(I32),
+            )

@@ -2,7 +2,7 @@ from contextlib import ExitStack
 
 import concourse.mybir as mybir
 
-K, T, S, N = 512, 2048, 512, 512
+T, S, N = 2048, 512, 512
 FLOPS = 3 * 2 * 512 * 512 * 512
 
 F32 = mybir.dt.float32
@@ -18,17 +18,26 @@ ACT = mybir.ActivationFunctionType
 
 P = 128
 PACK = 4
+LAST = PACK - 1
+BANKS = 8
 SPARE = 32
+HALF = S // 2
 CH = 128
 NCH = S // CH
+FUSED_TILES = 2
+SCALAR_CHUNK = 1
 
 
-def load_scale_rows(queue, tile_bytes, dram_rows):
+def load_scale_rows(queues, tile_bytes, dram_rows):
     for q in range(4):
-        queue.dma_start(
+        queues[q].dma_start(
             out=tile_bytes[32 * q : 32 * q + 4, :].bitcast(I32),
             in_=dram_rows[4 * q : 4 * q + 4, :].bitcast(I32),
         )
+
+
+def offsets(list_tile, first, count):
+    return list_tile[:, first // 16 : (first + count) // 16]
 
 
 def tile_picked_ybenesn_mul_po_kernel(
@@ -39,34 +48,50 @@ def tile_picked_ybenesn_mul_po_kernel(
     with ExitStack() as ctx:
         keep = ctx.enter_context(tc.tile_pool(name="keep", bufs=1))
         psum = ctx.enter_context(tc.psum_pool(name="psum", bufs=1))
+        all_sync = [nc.sync] * 4
+        halves = [slice(h * HALF, (h + 1) * HALF) for h in range(2)]
+        banks_taken = []
+
+        def next_bank(shape):
+            name = f"acc{len(banks_taken)}"
+            bank = psum.tile(shape, F32, name=name, tag=f"bank{len(banks_taken) % BANKS}")
+            banks_taken.append(name)
+            return bank
 
         offs_sb = keep.tile([P, S // 16], U16, name="offs_sb")
         s1_sb = keep.tile([P, S // 16], U16, name="s1_sb")
         s2_sb = keep.tile([P, S // 16], U16, name="s2_sb")
         xw_all = keep.tile([P, T], U32, name="xw_all", align_bytes=64)
         xs_all = keep.tile([P, T], U8, name="xs_all", align_bytes=64)
-        raw_words = [keep.tile([P, 2 * N], U8, name=f"raw_words{i}", align_bytes=64) for i in range(2)]
-        raw_scales = [keep.tile([P, N], U8, name=f"raw_scales{i}", align_bytes=64) for i in range(2)]
-        unit_sb = keep.tile([P, PACK], F32, name="unit_sb")
+        raw_words = [
+            keep.tile([P, 2 * N], U8, name=f"raw_words{i}", tag=f"raw_words{i}", align_bytes=64) for i in range(3)
+        ]
+        raw_scales = [keep.tile([P, N], U8, name=f"raw_scales{i}", align_bytes=64) for i in range(3)]
+        y_wins = [keep.tile([P, S + SPARE], F32, name=f"y_win{t}", tag=f"y_win{t}", align_bytes=64) for t in range(PACK)]
+        swap_wins = [keep.tile([P, S + SPARE], F32, name=f"swap_win{t}") for t in range(PACK)]
 
-        y_wins = [keep.tile([P, S + SPARE], F32, name=f"y_win{t}") for t in range(PACK)]
-        set_wins = [keep.tile([P, S + SPARE], F32, name=f"set_win{t}") for t in range(PACK)]
-        nc.vector.memset(xs_all[:].bitcast(I32), 0)
-        nc.vector.memset(raw_scales[0][:].bitcast(I32), 0)
-        for win in y_wins + set_wins:
-            nc.gpsimd.memset(win[:, S : S + SPARE], 0.0)
-        nc.gpsimd.dma_start(out=unit_sb[:], in_=unit.rearrange("(p t) o -> p (t o)", t=PACK))
-        nc.gpsimd.memset(raw_scales[1][:].bitcast(I32), 0)
-
+        xs_stage = keep.tile([P, T], U8, name="xs_stage", align_bytes=64)
+        load_scale_rows(all_sync, xs_stage, x_scales[0])
         nc.sync.dma_start(offs_sb[:], offs)
         nc.sync.dma_start(out=raw_words[0][:].bitcast(I32), in_=w1_words[0].bitcast(I32))
         nc.sync.dma_start(out=raw_words[1][:].bitcast(I32), in_=w2_words[0].bitcast(I32))
+        nc.sync.dma_start(out=xw_all[:].bitcast(I32), in_=x_words[0].rearrange("p n t -> p (n t)").bitcast(I32))
+        nc.gpsimd.dma_start(out=raw_words[2][:].bitcast(I32), in_=w3_words[0].bitcast(I32))
+
+        nc.vector.memset(xs_all[:].bitcast(I32), 0)
+        for raw in raw_scales:
+            nc.vector.memset(raw[:].bitcast(I32), 0)
+        for win in y_wins + swap_wins:
+            nc.vector.memset(win[:, S : S + SPARE], 0.0)
+
+        load_scale_rows(all_sync, raw_scales[0], w1_scales[0])
+        load_scale_rows([nc.sync] * 3 + [nc.gpsimd], raw_scales[1], w2_scales[0])
         nc.sync.dma_start(s1_sb[:], s1)
         nc.sync.dma_start(s2_sb[:], s2)
-        nc.sync.dma_start(out=xw_all[:].bitcast(I32), in_=x_words[0].rearrange("p n t -> p (n t)").bitcast(I32))
-        load_scale_rows(nc.scalar, xs_all, x_scales[0])
-        load_scale_rows(nc.sync, raw_scales[0], w1_scales[0])
-        load_scale_rows(nc.sync, raw_scales[1], w2_scales[0])
+        load_scale_rows(all_sync, raw_scales[2], w3_scales[0])
+        for q in range(4):
+            rows = slice(32 * q, 32 * q + 4)
+            nc.vector.tensor_copy(out=xs_all[rows, :].bitcast(I32), in_=xs_stage[rows, :].bitcast(I32))
 
         def deal_words(raw, name):
             dealt = keep.tile([P, 2 * N], U8, name=name, align_bytes=64)
@@ -76,13 +101,11 @@ def tile_picked_ybenesn_mul_po_kernel(
             )
             return dealt
 
-        def deal_scales(raw, name):
-            dealt = keep.tile([P, N], U8, name=name, align_bytes=64)
+        def deal_scales(dealt, raw, t0, t1):
             nc.vector.tensor_copy(
-                out=dealt[:].rearrange("p (t m) -> p t m", t=PACK),
-                in_=raw[:].rearrange("p (m t) -> p t m", t=PACK),
+                out=dealt[:, P * t0 : P * t1].rearrange("p (t m) -> p t m", m=P),
+                in_=raw[:].rearrange("p (m t) -> p t m", t=PACK)[:, t0:t1, :],
             )
-            return dealt
 
         w1w = deal_words(raw_words[0], "w1w")
         w2w = deal_words(raw_words[1], "w2w")
@@ -90,12 +113,17 @@ def tile_picked_ybenesn_mul_po_kernel(
         xw = keep.tile([P, S], U32, name="xw", align_bytes=64)
         xs = keep.tile([P, S], U8, name="xs", align_bytes=64)
         nc.vector.tensor_copy(xs[:], xs_all[:].indirect(offs_sb[:]))
-        w1s = deal_scales(raw_scales[0], "w1s")
-        nc.vector.tensor_copy(xw[:], xw_all[:].indirect(offs_sb[:]))
-        w2s = deal_scales(raw_scales[1], "w2s")
+        for cols in halves:
+            nc.vector.tensor_copy(xw[:, cols], xw_all[:].indirect(offsets(offs_sb, cols.start, HALF)))
 
-        nc.sync.dma_start(out=raw_words[0][:].bitcast(I32), in_=w3_words[0].bitcast(I32))
-        load_scale_rows(nc.sync, raw_scales[0], w3_scales[0])
+        w1s = keep.tile([P, N], U8, name="w1s", align_bytes=64)
+        w2s = keep.tile([P, N], U8, name="w2s", align_bytes=64)
+        for t0, t1 in ((0, 1), (1, PACK)):
+            deal_scales(w1s, raw_scales[0], t0, t1)
+            deal_scales(w2s, raw_scales[1], t0, t1)
+        w3w = deal_words(raw_words[2], "w3w")
+        unit_sb = keep.tile([P, PACK], F32, name="unit_sb", tag="raw_words1", align_bytes=64)
+        nc.sync.dma_start(out=unit_sb[:], in_=unit.rearrange("(p t) o -> p (t o)", t=PACK))
 
         def product(bank, words, scales, t, rhs, rhs_scale):
             nc.tensor.matmul_mx(
@@ -108,93 +136,125 @@ def tile_picked_ybenesn_mul_po_kernel(
                 stop=True,
             )
 
-        neg_lay2 = keep.tile([P, PACK, S], F32, name="neg_lay2")
-        picked = keep.tile([P, PACK, S], F32, name="picked")
-        w3w = None
-        w3s = None
-        for t in range(PACK):
-            yg_ps = psum.tile([P, S], F32, name=f"yg_ps{t}", tag=f"bank{2 * t}")
-            y_ps = psum.tile([P, S], F32, name=f"y_ps{t}", tag=f"bank{2 * t + 1}")
-            product(y_ps[:], w1w, w1s, t, xw[:], xs[:])
-            product(yg_ps[:], w2w, w2s, t, xw[:], xs[:])
+        lay2_wins = [keep.tile([P, 2 * S], F32, name=f"lay2_win{t}") for t in range(PACK)]
+        swap2s = [keep.tile([P, S], F32, name=f"swap2_{t}", tag=f"swap2_{t}") for t in range(PACK)]
+        lay1s = [keep.tile([P, S], F32, name=f"lay1_{t}") for t in range(PACK)]
+        picked = [keep.tile([P, S], F32, name=f"picked{t}") for t in range(PACK)]
+        sent_wins = []
 
-            y_win, set_win = y_wins[t], set_wins[t]
-            part_tile = keep.tile([P, S], F32, name=f"part{t}")
-            rest_win = keep.tile([P, 2 * S], F32, name=f"rest_win{t}")
-            last_win = keep.tile([P, 2 * S], F32, name=f"last_win{t}")
-            lay1 = keep.tile([P, S], F32, name=f"lay1_{t}")
-            kept = keep.tile([P, S], F32, name=f"kept{t}")
-            y, set1 = y_win[:, 0:S], set_win[:, 0:S]
-            y1, diff, part = last_win[:, S : 2 * S], rest_win[:, S : 2 * S], part_tile[:]
+        def products(t):
+            y_win, swap_win = y_wins[t], swap_wins[t]
+            for cols in halves if t == 0 else [slice(0, S)]:
+                y_ps = next_bank([P, cols.stop - cols.start])
+                product(y_ps[:], w1w, w1s, t, xw[:, cols], xs[:, cols])
+                nc.scalar.copy(out=y_win[:, cols], in_=y_ps[:])
+                if t > 0:
+                    nc.scalar.activation(lay2_wins[t][:, S : 2 * S], y_win[:].indirect(s1_sb[:]), ACT.Copy)
+                yg_ps = next_bank([P, cols.stop - cols.start])
+                product(yg_ps[:], w2w, w2s, t, xw[:, cols], xs[:, cols])
+                nc.scalar.activation(swap_win[:, cols], yg_ps[:], ACT.Sigmoid, scale=-1.5)
 
+        def gather_swap2(t):
+            nc.scalar.activation(swap2s[t][:], swap_wins[t][:].indirect(s2_sb[:]), ACT.Copy)
+
+        def layer1(t):
+            sent_win = keep.tile([P, 2 * S], F32, name=f"sent_win{t}", tag=f"sent_win{t % 2}")
+            sent_wins.append(sent_win)
+            y, swap = y_wins[t][:, 0:S], swap_wins[t][:, 0:S]
+            partner, term = lay2_wins[t][:, S : 2 * S], sent_win[:, S : 2 * S]
             if t == 0:
-                half = S // 2
-                nc.vector.tensor_copy(out=y, in_=y_ps[:])
-                nc.scalar.activation(set1, yg_ps[:], ACT.Sigmoid, scale=1.5)
-                nc.vector.tensor_copy(y1[:, 0:half], y_win[:].indirect(s1_sb[:, 0 : half // 16]))
-                nc.scalar.activation(y1[:, half:S], y_win[:].indirect(s1_sb[:, half // 16 : S // 16]), ACT.Copy)
+                for cols in halves:
+                    nc.vector.scalar_tensor_tensor(term[:, cols], swap[:, cols], 1.0, y[:, cols], ALU.subtract, ALU.mult)
+                nc.vector.tensor_tensor(partner, y_wins[t][:].indirect(s1_sb[:]), swap, ALU.mult)
+                nc.vector.tensor_tensor(lay1s[t][:], partner, term, ALU.subtract)
             else:
-                nc.scalar.copy(out=y, in_=y_ps[:])
-                nc.scalar.activation(y1, y_win[:].indirect(s1_sb[:]), ACT.Copy)
-                nc.scalar.activation(set1, yg_ps[:], ACT.Sigmoid, scale=1.5)
+                step = keep.tile([P, S], F32, name=f"step{t}", tag=f"step{t}")
+                nc.vector.tensor_tensor(term, partner, y, ALU.subtract)
+                nc.vector.tensor_tensor(step[:], term, swap, ALU.mult)
+                nc.vector.tensor_tensor(lay1s[t][:], step[:], y, ALU.add)
+            nc.vector.tensor_tensor(sent_win[:, 0:S], swap, lay1s[t][:], ALU.mult)
 
-            nc.vector.tensor_tensor(diff, y, y1, ALU.subtract)
-            nc.vector.tensor_tensor(part, diff, set1, ALU.mult)
-            nc.vector.tensor_tensor(lay1[:], part, y1, ALU.add)
-
-            nc.vector.scalar_tensor_tensor(rest_win[:, 0:S], set1, 1.0, lay1[:], ALU.subtract, ALU.mult)
-            if t == 0:
-                nc.vector.tensor_tensor(kept[:], set_win[:].indirect(s2_sb[:]), lay1[:], ALU.mult)
+        def layer2(t):
+            stay = keep.tile([P, S], F32, name=f"stay{t}", tag=f"step{LAST}" if t == LAST - 1 else f"stay{t}")
+            nc.vector.scalar_tensor_tensor(stay[:], swap2s[t][:], 1.0, lay1s[t][:], ALU.subtract, ALU.mult)
+            if t < FUSED_TILES:
+                nc.vector.tensor_tensor(lay2_wins[t][:, 0:S], sent_wins[t][:].indirect(s2_sb[:]), stay[:], ALU.subtract)
             else:
-                set2 = keep.tile([P, S], F32, name=f"set2_{t}")
-                nc.scalar.activation(set2[:], set_win[:].indirect(s2_sb[:]), ACT.Copy)
-                nc.vector.tensor_tensor(kept[:], set2[:], lay1[:], ALU.mult)
-            nc.vector.tensor_tensor(neg_lay2[:, t, :], rest_win[:].indirect(s2_sb[:]), kept[:], ALU.subtract)
-            nc.vector.tensor_scalar(last_win[:, 0:S], neg_lay2[:, t, :], -0.5, unit_sb[:, t : t + 1], ALU.add, ALU.mult)
-            width = CH if t == PACK - 1 else S
-            for c0 in range(0, S, width):
-                cols = s1_sb[:, c0 // 16 : (c0 + width) // 16]
-                nc.scalar.activation(picked[:, t, c0 : c0 + width], last_win[:].indirect(cols), ACT.Copy)
-            if t == 0:
-                w3w = deal_words(raw_words[0], "w3w")
-                w3s = deal_scales(raw_scales[0], "w3s")
+                came = keep.tile([P, S], F32, name=f"came{t}")
+                nc.scalar.activation(came[:], sent_wins[t][:].indirect(s2_sb[:]), ACT.Copy)
+                nc.vector.tensor_tensor(lay2_wins[t][:, 0:S], came[:], stay[:], ALU.subtract)
+
+        for t in range(PACK + 1):
+            if t < PACK:
+                products(t)
+            if t > 0:
+                gather_swap2(t - 1)
+            if t < PACK:
+                layer1(t)
+            if t > 0:
+                layer2(t - 1)
+
+        hid_rows = keep.tile([P, PACK, S], BF16, name="hid_rows", tag=f"swap2_{LAST}")
+
+        def pick(t, first, count):
+            cols = slice(first, first + count)
+            window = lay2_wins[t][:].indirect(offsets(s1_sb, first, count))
+            nc.scalar.activation(picked[t][:, cols], window, ACT.Copy, bias=0.5)
+
+        def hidden(t, first, count):
+            cols = slice(first, first + count)
+            nc.vector.scalar_tensor_tensor(
+                hid_rows[:, t, cols], picked[t][:, cols], unit_sb[:, t : t + 1], lay2_wins[t][:, cols],
+                ALU.mult, ALU.mult,
+            )
+
+        for t in range(LAST):
+            pick(t, 0, S)
+            hidden(t, 0, S)
+
+        w3s = keep.tile([P, N], U8, name="w3s", tag="y_win0", align_bytes=64)
+        deal_scales(w3s, raw_scales[2], 0, PACK)
 
         out_words = keep.tile([P, S], U32, name="out_words", align_bytes=64)
         out_scales = keep.tile([P, S], U8, name="out_scales", align_bytes=64)
         out_rows = out_0.rearrange("(p t) j -> p t j", t=PACK)
         out_word_rows = out_1[0].rearrange("p n t -> p (n t)").bitcast(I32)
+
+        def weave(copy, out, rows):
+            copy(
+                out=out.rearrange("p (g i t) -> p g t i", i=4, t=PACK),
+                in_=rows.rearrange("p t (g i) -> p g t i", i=4),
+            )
+
         results = []
         for c in range(NCH):
             cols = slice(c * CH, (c + 1) * CH)
+            pick(LAST, cols.start, CH)
+            hidden(LAST, cols.start, CH)
             hid = keep.tile([P, CH * PACK], BF16, name=f"hid{c}", align_bytes=64)
-            nc.vector.tensor_tensor(
-                hid[:].rearrange("p (g i t) -> p g t i", i=4, t=PACK),
-                picked[:, :, cols].rearrange("p t (g i) -> p g t i", i=4),
-                neg_lay2[:, :, cols].rearrange("p t (g i) -> p g t i", i=4),
-                ALU.mult,
-            )
+            weave(nc.scalar.copy if c == SCALAR_CHUNK else nc.vector.tensor_copy, hid[:], hid_rows[:, :, cols])
             hid_words = keep.tile([P, CH], U32, name=f"hid_words{c}", align_bytes=64)
             hid_scales = keep.tile([P, CH], U8, name=f"hid_scales{c}", align_bytes=64)
             nc.vector.quantize_mx(out=hid_words[:].bitcast(FP8X4), scales=hid_scales[:], in_=hid[:])
-            out_ps = psum.tile([P, PACK, CH], F32, name=f"out_ps{c}", tag=f"bank{c}")
+            out_ps = next_bank([P, PACK, CH])
             for t in range(PACK):
                 product(out_ps[:, t, :], w3w, w3s, t, hid_words[:], hid_scales[:])
-            out_f32 = keep.tile([P, PACK, CH], F32, name=f"out_f32_{c}")
-            nc.scalar.copy(out=out_f32[:], in_=out_ps[:])
-            nc.sync.dma_start(out=out_rows[:, :, cols], in_=out_f32[:])
-            results.append(out_f32)
+            results.append(out_ps)
+
         for c in range(NCH):
             cols = slice(c * CH, (c + 1) * CH)
-            out_f32 = results[c]
+            out_f32 = keep.tile([P, PACK, CH], F32, name=f"out_f32_{c}")
+            nc.scalar.copy(out=out_f32[:], in_=results[c][:])
+            nc.sync.dma_start(out=out_rows[:, :, cols], in_=out_f32[:])
             out_bf = keep.tile([P, CH * PACK], BF16, name=f"out_bf{c}", align_bytes=64)
-            nc.vector.tensor_copy(
-                out=out_bf[:].rearrange("p (g i t) -> p g t i", i=4, t=PACK),
-                in_=out_f32[:].rearrange("p t (g i) -> p g t i", i=4),
-            )
+            weave(nc.vector.tensor_copy, out_bf[:], out_f32[:])
             nc.vector.quantize_mx(out=out_words[:, cols].bitcast(FP8X4), scales=out_scales[:, cols], in_=out_bf[:])
-            nc.sync.dma_start(out=out_word_rows[:, cols], in_=out_words[:, cols].bitcast(I32))
+            if c >= NCH - 2:
+                done = slice(0, S - CH) if c == NCH - 2 else cols
+                nc.sync.dma_start(out=out_word_rows[:, done], in_=out_words[:, done].bitcast(I32))
         for q in range(4):
-            nc.sync.dma_start(
+            queue = nc.sync if q < 2 else nc.scalar
+            queue.dma_start(
                 out=out_2[0][4 * q : 4 * q + 4, :].bitcast(I32),
                 in_=out_scales[32 * q : 32 * q + 4, :].bitcast(I32),
             )

@@ -81,8 +81,9 @@ def tile_picked_ybenesn_mul_po_kernel(
         nc.vector.memset(xs_all[:].bitcast(I32), 0)
         for raw in raw_scales:
             nc.vector.memset(raw[:].bitcast(I32), 0)
-        for win in y_wins + swap_wins:
-            nc.vector.memset(win[:, S : S + SPARE], 0.0)
+        for y_win, swap_win in zip(y_wins, swap_wins):
+            nc.vector.memset(y_win[:, S : S + SPARE], 0.0)
+            nc.scalar.activation(swap_win[:, S : S + SPARE], y_win[:, S : S + SPARE], ACT.Sigmoid, scale=-1.5)
 
         load_scale_rows(all_sync, raw_scales[0], w1_scales[0])
         load_scale_rows([nc.sync] * 3 + [nc.gpsimd], raw_scales[1], w2_scales[0])

@@ -138,18 +138,21 @@ def tile_picked_ybenesn_mul_po_kernel(
             )
 
         lay2_wins = [keep.tile([P, 2 * S], F32, name=f"lay2_win{t}") for t in range(PACK)]
+        sent_wins = [keep.tile([P, 2 * S], F32, name=f"sent_win{t}") for t in range(PACK)]
         swap2s = [keep.tile([P, S], F32, name=f"swap2_{t}", tag=f"swap2_{t}") for t in range(PACK)]
         lay1s = [keep.tile([P, S], F32, name=f"lay1_{t}") for t in range(PACK)]
         picked = [keep.tile([P, S], F32, name=f"picked{t}") for t in range(PACK)]
-        sent_wins = []
+
+        def pieces(t):
+            return halves if t == 0 else [slice(0, S)]
 
         def products(t):
             y_win, swap_win = y_wins[t], swap_wins[t]
-            for cols in halves if t == 0 else [slice(0, S)]:
+            for cols in pieces(t):
                 y_ps = next_bank([P, cols.stop - cols.start])
                 product(y_ps[:], w1w, w1s, t, xw[:, cols], xs[:, cols])
                 nc.scalar.copy(out=y_win[:, cols], in_=y_ps[:])
-                if t > 0:
+                if t >= FUSED_TILES:
                     nc.scalar.activation(lay2_wins[t][:, S : 2 * S], y_win[:].indirect(s1_sb[:]), ACT.Copy)
                 yg_ps = next_bank([P, cols.stop - cols.start])
                 product(yg_ps[:], w2w, w2s, t, xw[:, cols], xs[:, cols])
@@ -159,12 +162,11 @@ def tile_picked_ybenesn_mul_po_kernel(
             nc.scalar.activation(swap2s[t][:], swap_wins[t][:].indirect(s2_sb[:]), ACT.Copy)
 
         def layer1(t):
-            sent_win = keep.tile([P, 2 * S], F32, name=f"sent_win{t}", tag=f"sent_win{t % 2}")
-            sent_wins.append(sent_win)
+            sent_win = sent_wins[t]
             y, swap = y_wins[t][:, 0:S], swap_wins[t][:, 0:S]
             partner, term = lay2_wins[t][:, S : 2 * S], sent_win[:, S : 2 * S]
-            if t == 0:
-                for cols in halves:
+            if t < FUSED_TILES:
+                for cols in pieces(t):
                     nc.vector.scalar_tensor_tensor(term[:, cols], swap[:, cols], 1.0, y[:, cols], ALU.subtract, ALU.mult)
                 nc.vector.tensor_tensor(partner, y_wins[t][:].indirect(s1_sb[:]), swap, ALU.mult)
                 nc.vector.tensor_tensor(lay1s[t][:], partner, term, ALU.subtract)
@@ -176,7 +178,8 @@ def tile_picked_ybenesn_mul_po_kernel(
             nc.vector.tensor_tensor(sent_win[:, 0:S], swap, lay1s[t][:], ALU.mult)
 
         def layer2(t):
-            stay = keep.tile([P, S], F32, name=f"stay{t}", tag=f"step{LAST}" if t == LAST - 1 else f"stay{t}")
+            has_step = FUSED_TILES <= t + 1 <= LAST
+            stay = keep.tile([P, S], F32, name=f"stay{t}", tag=f"step{t + 1}" if has_step else f"stay{t}")
             nc.vector.scalar_tensor_tensor(stay[:], swap2s[t][:], 1.0, lay1s[t][:], ALU.subtract, ALU.mult)
             if t < FUSED_TILES:
                 nc.vector.tensor_tensor(lay2_wins[t][:, 0:S], sent_wins[t][:].indirect(s2_sb[:]), stay[:], ALU.subtract)

from contextlib import ExitStack

import concourse.mybir as mybir

T, S, N = 2048, 512, 512
FLOPS = 3 * 2 * 512 * 512 * 512

F32 = mybir.dt.float32
BF16 = mybir.dt.bfloat16
I32 = mybir.dt.int32
U32 = mybir.dt.uint32
U16 = mybir.dt.uint16
U8 = mybir.dt.uint8
FP8X4 = mybir.dt.float8_e4m3fn_x4
FP4X4 = mybir.dt.float4_e2m1fn_x4
ALU = mybir.AluOpType
ACT = mybir.ActivationFunctionType

P = 128
PACK = 4
LAST = PACK - 1
BANKS = 8
SPARE = 32
HALF = S // 2
CH = 128
NCH = S // CH
FUSED_TILES = 2
SCALAR_CHUNK = 1


def load_scale_rows(queues, tile_bytes, dram_rows):
    for q in range(4):
        queues[q].dma_start(
            out=tile_bytes[32 * q : 32 * q + 4, :].bitcast(I32),
            in_=dram_rows[4 * q : 4 * q + 4, :].bitcast(I32),
        )


def offsets(list_tile, first, count):
    return list_tile[:, first // 16 : (first + count) // 16]


def tile_picked_ybenesn_mul_po_kernel(
    tc, x_words, x_scales, w1_words, w1_scales, w2_words, w2_scales, unit, w3_words, w3_scales, offs, s1, s2,
    out_0, out_1, out_2,
):
    nc = tc.nc
    with ExitStack() as ctx:
        keep = ctx.enter_context(tc.tile_pool(name="keep", bufs=1))
        psum = ctx.enter_context(tc.psum_pool(name="psum", bufs=1))
        all_sync = [nc.sync] * 4
        halves = [slice(h * HALF, (h + 1) * HALF) for h in range(2)]
        banks_taken = []

        def next_bank(shape):
            name = f"acc{len(banks_taken)}"
            bank = psum.tile(shape, F32, name=name, tag=f"bank{len(banks_taken) % BANKS}")
            banks_taken.append(name)
            return bank

        offs_sb = keep.tile([P, S // 16], U16, name="offs_sb")
        s1_sb = keep.tile([P, S // 16], U16, name="s1_sb")
        s2_sb = keep.tile([P, S // 16], U16, name="s2_sb")
        xw_all = keep.tile([P, T], U32, name="xw_all", align_bytes=64)
        xs_all = keep.tile([P, T], U8, name="xs_all", align_bytes=64)
        raw_words = [
            keep.tile([P, 2 * N], U8, name=f"raw_words{i}", tag=f"raw_words{i}", align_bytes=64) for i in range(3)
        ]
        raw_scales = [keep.tile([P, N], U8, name=f"raw_scales{i}", align_bytes=64) for i in range(3)]
        y_wins = [keep.tile([P, S + SPARE], F32, name=f"y_win{t}", tag=f"y_win{t}", align_bytes=64) for t in range(PACK)]
        swap_wins = [keep.tile([P, S + SPARE], F32, name=f"swap_win{t}") for t in range(PACK)]

        xs_stage = keep.tile([P, T], U8, name="xs_stage", align_bytes=64)
        load_scale_rows(all_sync, xs_stage, x_scales[0])
        nc.sync.dma_start(offs_sb[:], offs)
        nc.sync.dma_start(out=raw_words[0][:].bitcast(I32), in_=w1_words[0].bitcast(I32))
        nc.sync.dma_start(out=raw_words[1][:].bitcast(I32), in_=w2_words[0].bitcast(I32))
        nc.sync.dma_start(out=xw_all[:].bitcast(I32), in_=x_words[0].rearrange("p n t -> p (n t)").bitcast(I32))
        nc.gpsimd.dma_start(out=raw_words[2][:].bitcast(I32), in_=w3_words[0].bitcast(I32))

        nc.vector.memset(xs_all[:].bitcast(I32), 0)
        for raw in raw_scales:
            nc.vector.memset(raw[:].bitcast(I32), 0)
        for y_win, swap_win in zip(y_wins, swap_wins):
            nc.vector.memset(y_win[:, S : S + SPARE], 0.0)
            nc.scalar.activation(swap_win[:, S : S + SPARE], y_win[:, S : S + SPARE], ACT.Sigmoid, scale=-1.5)

        load_scale_rows(all_sync, raw_scales[0], w1_scales[0])
        load_scale_rows([nc.sync] * 3 + [nc.gpsimd], raw_scales[1], w2_scales[0])
        nc.sync.dma_start(s1_sb[:], s1)
        nc.sync.dma_start(s2_sb[:], s2)
        load_scale_rows(all_sync, raw_scales[2], w3_scales[0])
        for q in range(4):
            rows = slice(32 * q, 32 * q + 4)
            nc.vector.tensor_copy(out=xs_all[rows, :].bitcast(I32), in_=xs_stage[rows, :].bitcast(I32))

        def deal_words(raw, name):
            dealt = keep.tile([P, 2 * N], U8, name=name, align_bytes=64)
            nc.scalar.copy(
                out=dealt[:].bitcast(U16).rearrange("p (t m) -> p t m", t=PACK),
                in_=raw[:].bitcast(U16).rearrange("p (m t) -> p t m", t=PACK),
            )
            return dealt

        def deal_scales(dealt, raw, t0, t1):
            nc.vector.tensor_copy(
                out=dealt[:, P * t0 : P * t1].rearrange("p (t m) -> p t m", m=P),
                in_=raw[:].rearrange("p (m t) -> p t m", t=PACK)[:, t0:t1, :],
            )

        w1w = deal_words(raw_words[0], "w1w")
        w2w = deal_words(raw_words[1], "w2w")

        xw = keep.tile([P, S], U32, name="xw", align_bytes=64)
        xs = keep.tile([P, S], U8, name="xs", align_bytes=64)
        nc.vector.tensor_copy(xs[:], xs_all[:].indirect(offs_sb[:]))
        for cols in halves:
            nc.vector.tensor_copy(xw[:, cols], xw_all[:].indirect(offsets(offs_sb, cols.start, HALF)))

        w1s = keep.tile([P, N], U8, name="w1s", align_bytes=64)
        w2s = keep.tile([P, N], U8, name="w2s", align_bytes=64)
        for t0, t1 in ((0, 1), (1, PACK)):
            deal_scales(w1s, raw_scales[0], t0, t1)
            deal_scales(w2s, raw_scales[1], t0, t1)
        w3w = deal_words(raw_words[2], "w3w")
        unit_sb = keep.tile([P, PACK], F32, name="unit_sb", tag="raw_words1", align_bytes=64)
        nc.sync.dma_start(out=unit_sb[:], in_=unit.rearrange("(p t) o -> p (t o)", t=PACK))

        def product(bank, words, scales, t, rhs, rhs_scale):
            nc.tensor.matmul_mx(
                out=bank,
                lhsT=words[:, 2 * P * t : 2 * P * (t + 1)].bitcast(FP4X4),
                lhsT_scale=scales[:, P * t : P * (t + 1)],
                rhs=rhs.bitcast(FP8X4),
                rhs_scale=rhs_scale,
                start=True,
                stop=True,
            )

        lay2_wins = [keep.tile([P, 2 * S], F32, name=f"lay2_win{t}") for t in range(PACK)]
        sent_wins = [keep.tile([P, 2 * S], F32, name=f"sent_win{t}") for t in range(PACK)]
        swap2s = [keep.tile([P, S], F32, name=f"swap2_{t}", tag=f"swap2_{t}") for t in range(PACK)]
        lay1s = [keep.tile([P, S], F32, name=f"lay1_{t}") for t in range(PACK)]
        picked = [keep.tile([P, S], F32, name=f"picked{t}") for t in range(PACK)]

        def pieces(t):
            return halves if t == 0 else [slice(0, S)]

        def products(t):
            y_win, swap_win = y_wins[t], swap_wins[t]
            for cols in pieces(t):
                y_ps = next_bank([P, cols.stop - cols.start])
                product(y_ps[:], w1w, w1s, t, xw[:, cols], xs[:, cols])
                nc.scalar.copy(out=y_win[:, cols], in_=y_ps[:])
                if t >= FUSED_TILES:
                    nc.scalar.activation(lay2_wins[t][:, S : 2 * S], y_win[:].indirect(s1_sb[:]), ACT.Copy)
                yg_ps = next_bank([P, cols.stop - cols.start])
                product(yg_ps[:], w2w, w2s, t, xw[:, cols], xs[:, cols])
                nc.scalar.activation(swap_win[:, cols], yg_ps[:], ACT.Sigmoid, scale=-1.5)

        def gather_swap2(t):
            nc.scalar.activation(swap2s[t][:], swap_wins[t][:].indirect(s2_sb[:]), ACT.Copy)

        def layer1(t):
            sent_win = sent_wins[t]
            y, swap = y_wins[t][:, 0:S], swap_wins[t][:, 0:S]
            partner, term = lay2_wins[t][:, S : 2 * S], sent_win[:, S : 2 * S]
            if t < FUSED_TILES:
                for cols in pieces(t):
                    nc.vector.scalar_tensor_tensor(term[:, cols], swap[:, cols], 1.0, y[:, cols], ALU.subtract, ALU.mult)
                nc.vector.tensor_tensor(partner, y_wins[t][:].indirect(s1_sb[:]), swap, ALU.mult)
                nc.vector.tensor_tensor(lay1s[t][:], partner, term, ALU.subtract)
            else:
                step = keep.tile([P, S], F32, name=f"step{t}", tag=f"step{t}")
                nc.vector.tensor_tensor(term, partner, y, ALU.subtract)
                nc.vector.tensor_tensor(step[:], term, swap, ALU.mult)
                nc.vector.tensor_tensor(lay1s[t][:], step[:], y, ALU.add)
            nc.vector.tensor_tensor(sent_win[:, 0:S], swap, lay1s[t][:], ALU.mult)

        def layer2(t):
            has_step = FUSED_TILES <= t + 1 <= LAST
            stay = keep.tile([P, S], F32, name=f"stay{t}", tag=f"step{t + 1}" if has_step else f"stay{t}")
            nc.vector.scalar_tensor_tensor(stay[:], swap2s[t][:], 1.0, lay1s[t][:], ALU.subtract, ALU.mult)
            if t < FUSED_TILES:
                nc.vector.tensor_tensor(lay2_wins[t][:, 0:S], sent_wins[t][:].indirect(s2_sb[:]), stay[:], ALU.subtract)
            else:
                came = keep.tile([P, S], F32, name=f"came{t}")
                nc.scalar.activation(came[:], sent_wins[t][:].indirect(s2_sb[:]), ACT.Copy)
                nc.vector.tensor_tensor(lay2_wins[t][:, 0:S], came[:], stay[:], ALU.subtract)

        for t in range(PACK + 1):
            if t < PACK:
                products(t)
            if t > 0:
                gather_swap2(t - 1)
            if t < PACK:
                layer1(t)
            if t > 0:
                layer2(t - 1)

        hid_rows = keep.tile([P, PACK, S], BF16, name="hid_rows", tag=f"swap2_{LAST}")

        def pick(t, first, count):
            cols = slice(first, first + count)
            window = lay2_wins[t][:].indirect(offsets(s1_sb, first, count))
            nc.scalar.activation(picked[t][:, cols], window, ACT.Copy, bias=0.5)

        def hidden(t, first, count):
            cols = slice(first, first + count)
            nc.vector.scalar_tensor_tensor(
                hid_rows[:, t, cols], picked[t][:, cols], unit_sb[:, t : t + 1], lay2_wins[t][:, cols],
                ALU.mult, ALU.mult,
            )

        for t in range(LAST):
            pick(t, 0, S)
            hidden(t, 0, S)

        w3s = keep.tile([P, N], U8, name="w3s", tag="y_win0", align_bytes=64)
        deal_scales(w3s, raw_scales[2], 0, PACK)

        out_words = keep.tile([P, S], U32, name="out_words", align_bytes=64)
        out_scales = keep.tile([P, S], U8, name="out_scales", align_bytes=64)
        out_rows = out_0.rearrange("(p t) j -> p t j", t=PACK)
        out_word_rows = out_1[0].rearrange("p n t -> p (n t)").bitcast(I32)

        def weave(copy, out, rows):
            copy(
                out=out.rearrange("p (g i t) -> p g t i", i=4, t=PACK),
                in_=rows.rearrange("p t (g i) -> p g t i", i=4),
            )

        results = []
        for c in range(NCH):
            cols = slice(c * CH, (c + 1) * CH)
            pick(LAST, cols.start, CH)
            hidden(LAST, cols.start, CH)
            hid = keep.tile([P, CH * PACK], BF16, name=f"hid{c}", align_bytes=64)
            weave(nc.scalar.copy if c == SCALAR_CHUNK else nc.vector.tensor_copy, hid[:], hid_rows[:, :, cols])
            hid_words = keep.tile([P, CH], U32, name=f"hid_words{c}", align_bytes=64)
            hid_scales = keep.tile([P, CH], U8, name=f"hid_scales{c}", align_bytes=64)
            nc.vector.quantize_mx(out=hid_words[:].bitcast(FP8X4), scales=hid_scales[:], in_=hid[:])
            out_ps = next_bank([P, PACK, CH])
            for t in range(PACK):
                product(out_ps[:, t, :], w3w, w3s, t, hid_words[:], hid_scales[:])
            results.append(out_ps)

        for c in range(NCH):
            cols = slice(c * CH, (c + 1) * CH)
            out_f32 = keep.tile([P, PACK, CH], F32, name=f"out_f32_{c}")
            nc.scalar.copy(out=out_f32[:], in_=results[c][:])
            nc.sync.dma_start(out=out_rows[:, :, cols], in_=out_f32[:])
            out_bf = keep.tile([P, CH * PACK], BF16, name=f"out_bf{c}", align_bytes=64)
            weave(nc.vector.tensor_copy, out_bf[:], out_f32[:])
            nc.vector.quantize_mx(out=out_words[:, cols].bitcast(FP8X4), scales=out_scales[:, cols], in_=out_bf[:])
            if c >= NCH - 2:
                done = slice(0, S - CH) if c == NCH - 2 else cols
                nc.sync.dma_start(out=out_word_rows[:, done], in_=out_words[:, done].bitcast(I32))
        for q in range(4):
            queue = nc.sync if q < 2 else nc.scalar
            queue.dma_start(
                out=out_2[0][4 * q : 4 * q + 4, :].bitcast(I32),
                in_=out_scales[32 * q : 32 * q + 4, :].bitcast(I32),
            )
